import numpy as np
import ml_dtypes


def mxq(x, axis, fmt="e4m3"):
    dtype, down = {"e4m3": (ml_dtypes.float8_e4m3fn, 7), "e5m2": (ml_dtypes.float8_e5m2, 14)}[fmt]
    v = np.moveaxis(np.asarray(x, np.float32).astype(ml_dtypes.bfloat16).astype(np.float64), axis, -1)
    blocks = v.reshape(v.shape[:-1] + (-1, 32))
    amax = np.abs(blocks).max(-1, keepdims=True)
    byte = np.maximum(np.where(amax > 0, np.frexp(amax)[1] - 1 + 127, 0) - down, 1)
    scale = np.exp2(byte - 127.0)
    codes = (blocks / scale).astype(np.float32).astype(dtype).astype(np.float64)
    return np.moveaxis((codes * scale).reshape(v.shape), -1, axis)


WIDE = False


def mx_kscale(k):
    if not WIDE:
        return np.ones(k)
    levels = np.array([10, -10, 5, -5, 0])
    if k % 512:
        return np.exp2(np.random.permutation(np.resize(levels, k // 32))).repeat(32)
    a = np.empty((k // 512, 16))
    for p in range(k // 512):
        a[p, :8] = np.random.permutation(np.resize(levels, 8))
        for g in range(8):
            far = levels[np.abs(levels - a[p, g]) >= 10]
            a[p, g + 8] = far[np.random.randint(len(far))]
    return np.exp2(a.ravel()).repeat(32)


def f64(x):
    return np.asarray(x).astype(np.float64)


def striped(idx):
    return np.tile(idx.reshape(-1, 16).T, (8, 1)).astype(np.uint16)


def unstriped(offs):
    return offs[:16].T.reshape(-1).astype(np.int64)


E2M1 = np.array([0.0, 0.5, 1.0, 1.5, 2.0, 3.0, 4.0, 6.0, -0.0, -0.5, -1.0, -1.5, -2.0, -3.0, -4.0, -6.0])


def pack_weight(w, fmt):
    k, n = w.shape
    w = f64(np.asarray(w, np.float32).astype(ml_dtypes.bfloat16)).reshape(k // 32, 32, n)
    amax = np.abs(w).max(1)
    if fmt == "e4m3":
        byte = np.frexp(amax)[1] - 1 + 127 - 7
    else:
        mant, ex = np.frexp(amax / 6.0)
        byte = np.where(mant > 0.5, ex, ex - 1) + 127
    byte = np.clip(np.where(amax > 0, byte, 1), 1, 254)
    scaled = (w * np.exp2(127.0 - byte)[:, None, :]).reshape(k, n).astype(np.float32)
    by_word = np.ascontiguousarray(scaled.reshape(k // 512, 128, 4, n).transpose(0, 1, 3, 2))
    if fmt == "e4m3":
        words = by_word.astype(ml_dtypes.float8_e4m3fn).view(np.uint8)
    else:
        c = by_word.astype(ml_dtypes.float4_e2m1fn).view(np.uint8) & 0xF
        words = (c[..., 0::2] | (c[..., 1::2] << 4)).reshape(k // 512, 128, 2 * n)
    return np.ascontiguousarray(words), np.ascontiguousarray(byte.astype(np.uint8).reshape(k // 512, 16, n))


def unpack_weight(words, scales, fmt):
    g, _, n = scales.shape
    words = np.ascontiguousarray(words).reshape(g, 128, n, -1)
    if fmt == "e4m3":
        vals = words.view(ml_dtypes.float8_e4m3fn).astype(np.float64)
    else:
        nib = np.empty((g, 128, n, 4), np.uint8)
        nib[..., 0::2] = words & 0xF
        nib[..., 1::2] = words >> 4
        vals = E2M1[nib]
    vals = vals * np.repeat(np.exp2(scales.astype(np.float64) - 127.0), 8, axis=1)[..., None]
    return vals.transpose(0, 1, 3, 2).reshape(g * 512, n)


def gelu(v):
    return 0.5 * v * (1.0 + np.tanh(np.sqrt(2.0 / np.pi) * (v + 0.044715 * v**3)))


K, M, T, S = 512, 128, 2048, 1024


def setup_inputs():
    n = np.random.standard_normal
    s = mx_kscale(K)[:, None]
    u = mx_kscale(512)[:, None]
    v = pack_weight(n((K, T)) * s, "e4m3")
    p_w2 = pack_weight(1.4 * n((512, M)) / np.sqrt(512) / u, "e2m1")
    return {
        "tab_words": v[0],
        "tab_scales": v[1],
        "w1": (n((K, 512)) / np.sqrt(K) / s * u.T).astype(np.float32),
        "w2_words": p_w2[0],
        "w2_scales": p_w2[1],
        "rT": n((M, T)).astype(np.float32),
        "b": (0.3 * n(128)).astype(np.float32),
        "offs": striped(np.random.permutation(T)[:S]),
    }


def reference(tab_words, tab_scales, w1, w2_words, w2_scales, rT, b, offs):
    tab_ = unpack_weight(tab_words, tab_scales, "e4m3")[:, unstriped(offs)]
    w1_ = mxq(f64(w1), 0, "e4m3")
    w2_ = unpack_weight(w2_words, w2_scales, "e2m1")
    h_ = mxq(np.maximum(w1_.T @ tab_, 0.0), 0, "e4m3")
    y = w2_.T @ h_
    return (gelu(y + f64(b)[:, None])) + f64(rT)[:, unstriped(offs)]

@@ -1,0 +1,114 @@
+from contextlib import ExitStack
+
+import concourse.mybir as mybir
+
+K, H, M, T, S = 512, 512, 128, 2048, 1024
+FLOPS = 2 * K * H * S + 2 * H * M * S
+
+F32 = mybir.dt.float32
+BF16 = mybir.dt.bfloat16
+I32 = mybir.dt.int32
+U32 = mybir.dt.uint32
+U16 = mybir.dt.uint16
+U8 = mybir.dt.uint8
+FP8X4 = mybir.dt.float8_e4m3fn_x4
+FP4X4 = mybir.dt.float4_e2m1fn_x4
+ACT = mybir.ActivationFunctionType
+ADD = mybir.AluOpType.add
+
+P = 128
+PACK = 4
+CH = 128
+GROUPS = [256,256,256,256]
+
+
+def tile_list_tabres_gelu_kernel(tc, tab_words, tab_scales, w1, w2_words, w2_scales, rT, b, offs, out):
+    nc = tc.nc
+    with ExitStack() as ctx:
+        keep = ctx.enter_context(tc.tile_pool(name="keep", bufs=1))
+        hps = ctx.enter_context(tc.psum_pool(name="hps", bufs=6))
+        yps = ctx.enter_context(tc.psum_pool(name="yps", bufs=2))
+
+        offsets = keep.tile([P, S // 16], U16, name="offsets")
+        words_win = keep.tile([P, T], I32, name="words_win", align_bytes=64)
+        scales_win = keep.tile([P, T // 4], I32, name="scales_win", align_bytes=64)
+        res_win = keep.tile([P, T], F32, name="res_win", align_bytes=64)
+        w1_raw = [keep.tile([P, PACK, H // 2], F32, name=f"w1_raw{u}") for u in range(2)]
+        w1_bf = keep.tile([P, PACK * H], BF16, name="w1_bf", align_bytes=64)
+        w1_codes = keep.tile([P, H], U32, name="w1_codes", align_bytes=64)
+        w1_sc = keep.tile([P, H], U8, name="w1_sc", align_bytes=64)
+        w2_codes = keep.tile([P, 2 * M], U8, name="w2_codes", align_bytes=64)
+        w2_sc = keep.tile([P, M], U8, name="w2_sc", align_bytes=64)
+        bias = keep.tile([P, 1], F32, name="bias")
+        warm = keep.tile([P, 1], F32, name="warm")
+        warm2 = keep.tile([P, 1], F32, name="warm2")
+        x_codes = keep.tile([P, S], U32, name="x_codes", align_bytes=64)
+        x_sc = keep.tile([P, S], U8, name="x_sc", align_bytes=64)
+        h_bf = keep.tile([P, PACK * S], BF16, name="h_bf", align_bytes=64)
+        h_codes = keep.tile([P, S], U32, name="h_codes", align_bytes=64)
+        h_sc = keep.tile([P, S], U8, name="h_sc", align_bytes=64)
+        res = keep.tile([P, S], F32, name="res", align_bytes=64)
+        act = keep.tile([P, S], F32, name="act", align_bytes=64)
+        fin = keep.tile([P, S], F32, name="fin", align_bytes=64)
+
+        nc.vector.memset(scales_win[:], 0)
+        nc.gpsimd.memset(warm[:], 0.0)
+        nc.gpsimd.memset(w2_sc[:], 0)
+        nc.scalar.activation(warm2[:], warm[:], ACT.Gelu_apprx_tanh)
+
+        nc.sync.dma_start(offsets[:], offs)
+        nc.sync.dma_start(w2_codes[:].bitcast(I32), w2_words[0].bitcast(I32))
+        with nc.allow_non_contiguous_dma(reason="one bias value a partition"):
+            nc.sync.dma_start(bias[:], b.rearrange("(p o) -> p o", o=1))
+        for r in range(4):
+            nc.sync.dma_start(scales_win[r:P:32, :], tab_scales[0, r:16:4, :].bitcast(I32))
+        w1_rows = w1.rearrange("(p j) c -> p j c", j=PACK)
+        for u in range(2):
+            nc.sync.dma_start(w1_raw[u][:], w1_rows[:, :, u * (H // 2):(u + 1) * (H // 2)])
+        nc.sync.dma_start(words_win[:], tab_words[0].rearrange("p t i -> p (t i)").bitcast(I32))
+        nc.sync.dma_start(res_win[:], rT)
+        for r in range(4):
+            nc.sync.dma_start(w2_sc[:].bitcast(I32)[r:P:32, :], w2_scales[0, r:16:4, :].bitcast(I32))
+
+        nc.vector.tensor_copy(x_sc[:], scales_win[:].bitcast(U8).indirect(offsets[:]))
+
+        w1_view = w1_bf[:].rearrange("p (t m j) -> p m t j", t=PACK, j=PACK)
+        for u in range(2):
+            nc.scalar.copy(w1_view[:, u * 64:(u + 1) * 64], w1_raw[u][:].rearrange("p j (m t) -> p m t j", t=PACK))
+        nc.vector.quantize_mx(out=w1_codes[:].bitcast(FP8X4), scales=w1_sc[:], in_=w1_bf[:])
+
+        def gather_words(lo, hi):
+            nc.vector.tensor_copy(x_codes[:, lo:hi], words_win[:].bitcast(U32).indirect(offsets[:, lo // 16:hi // 16]))
+
+        def gather_res(lo, hi):
+            nc.vector.tensor_copy(res[:, lo:hi], res_win[:].indirect(offsets[:, lo // 16:hi // 16]))
+
+        def layer1(lo):
+            bank = hps.tile([P, PACK, CH], F32, name="hbank")
+            for t in range(PACK):
+                nc.tensor.matmul_mx(out=bank[:, t, :], lhsT=w1_codes[:, t * P:(t + 1) * P].bitcast(FP8X4), lhsT_scale=w1_sc[:, t * P:(t + 1) * P],
+                                    rhs=x_codes[:, lo:lo + CH].bitcast(FP8X4), rhs_scale=x_sc[:, lo:lo + CH], start=True, stop=True)
+            nc.scalar.activation(h_bf[:, PACK * lo:PACK * (lo + CH)].rearrange("p (n t) -> p n t", t=PACK),
+                                 bank[:].rearrange("p t n -> p n t"), ACT.Relu)
+
+        def layer2(lo, hi):
+            nc.vector.quantize_mx(out=h_codes[:, lo:hi].bitcast(FP8X4), scales=h_sc[:, lo:hi], in_=h_bf[:, PACK * lo:PACK * hi])
+            ybank = yps.tile([P, hi - lo], F32, name="ybank")
+            nc.tensor.matmul_mx(out=ybank[:], lhsT=w2_codes[:].bitcast(FP4X4), lhsT_scale=w2_sc[:],
+                                rhs=h_codes[:, lo:hi].bitcast(FP8X4), rhs_scale=h_sc[:, lo:hi], start=True, stop=True)
+            nc.scalar.activation(act[:, lo:hi], ybank[:], ACT.Gelu_apprx_tanh, bias=bias[:])
+
+        def finish(lo, hi):
+            nc.vector.tensor_tensor(fin[:, lo:hi], act[:, lo:hi], res[:, lo:hi], ADD)
+            nc.sync.dma_start(out[:, lo:hi], fin[:, lo:hi])
+
+        for g in range(4):
+            gather_words(256 * g, 256 * (g + 1))
+            layer1(256 * g)
+            layer1(256 * g + CH)
+        for g in range(4):
+            layer2(256 * g, 256 * (g + 1))
+        for g in range(4):
+            gather_res(256 * g, 256 * (g + 1))
+        for g in range(4):
+            finish(256 * g, 256 * (g + 1))

@@ -26,8 +26,7 @@ def tile_list_tabres_gelu_kernel(tc, tab_words, tab_scales, w1, w2_words, w2_sca
     nc = tc.nc
     with ExitStack() as ctx:
         keep = ctx.enter_context(tc.tile_pool(name="keep", bufs=1))
-        hps = ctx.enter_context(tc.psum_pool(name="hps", bufs=6))
-        yps = ctx.enter_context(tc.psum_pool(name="yps", bufs=2))
+        banks = ctx.enter_context(tc.psum_pool(name="banks", bufs=8))
 
         offsets = keep.tile([P, S // 16], U16, name="offsets")
         words_win = keep.tile([P, T], I32, name="words_win", align_bytes=64)
@@ -45,7 +44,6 @@ def tile_list_tabres_gelu_kernel(tc, tab_words, tab_scales, w1, w2_words, w2_sca
         x_codes = keep.tile([P, S], U32, name="x_codes", align_bytes=64)
         x_sc = keep.tile([P, S], U8, name="x_sc", align_bytes=64)
         h_bf = keep.tile([P, PACK * S], BF16, name="h_bf", align_bytes=64)
-        h_codes = keep.tile([P, S], U32, name="h_codes", align_bytes=64)
         h_sc = keep.tile([P, S], U8, name="h_sc", align_bytes=64)
         res = keep.tile([P, S], F32, name="res", align_bytes=64)
         act = keep.tile([P, S], F32, name="act", align_bytes=64)
@@ -57,9 +55,6 @@ def tile_list_tabres_gelu_kernel(tc, tab_words, tab_scales, w1, w2_words, w2_sca
         nc.scalar.activation(warm2[:], warm[:], ACT.Gelu_apprx_tanh)
 
         nc.sync.dma_start(offsets[:], offs)
-        nc.sync.dma_start(w2_codes[:].bitcast(I32), w2_words[0].bitcast(I32))
-        with nc.allow_non_contiguous_dma(reason="one bias value a partition"):
-            nc.sync.dma_start(bias[:], b.rearrange("(p o) -> p o", o=1))
         for r in range(4):
             nc.sync.dma_start(scales_win[r:P:32, :], tab_scales[0, r:16:4, :].bitcast(I32))
         w1_rows = w1.rearrange("(p j) c -> p j c", j=PACK)
@@ -67,6 +62,9 @@ def tile_list_tabres_gelu_kernel(tc, tab_words, tab_scales, w1, w2_words, w2_sca
             nc.sync.dma_start(w1_raw[u][:], w1_rows[:, :, u * (H // 2):(u + 1) * (H // 2)])
         nc.sync.dma_start(words_win[:], tab_words[0].rearrange("p t i -> p (t i)").bitcast(I32))
         nc.sync.dma_start(res_win[:], rT)
+        nc.sync.dma_start(w2_codes[:].bitcast(I32), w2_words[0].bitcast(I32))
+        with nc.allow_non_contiguous_dma(reason="one bias value a partition"):
+            nc.sync.dma_start(bias[:], b.rearrange("(p o) -> p o", o=1))
         for r in range(4):
             nc.sync.dma_start(w2_sc[:].bitcast(I32)[r:P:32, :], w2_scales[0, r:16:4, :].bitcast(I32))
 
@@ -84,31 +82,32 @@ def tile_list_tabres_gelu_kernel(tc, tab_words, tab_scales, w1, w2_words, w2_sca
             nc.vector.tensor_copy(res[:, lo:hi], res_win[:].indirect(offsets[:, lo // 16:hi // 16]))
 
         def layer1(lo):
-            bank = hps.tile([P, PACK, CH], F32, name="hbank")
+            bank = banks.tile([P, PACK, CH], F32, name="hbank", tag="bank")
             for t in range(PACK):
                 nc.tensor.matmul_mx(out=bank[:, t, :], lhsT=w1_codes[:, t * P:(t + 1) * P].bitcast(FP8X4), lhsT_scale=w1_sc[:, t * P:(t + 1) * P],
                                     rhs=x_codes[:, lo:lo + CH].bitcast(FP8X4), rhs_scale=x_sc[:, lo:lo + CH], start=True, stop=True)
             nc.scalar.activation(h_bf[:, PACK * lo:PACK * (lo + CH)].rearrange("p (n t) -> p n t", t=PACK),
                                  bank[:].rearrange("p t n -> p n t"), ACT.Relu)
 
-        def layer2(lo, hi):
-            nc.vector.quantize_mx(out=h_codes[:, lo:hi].bitcast(FP8X4), scales=h_sc[:, lo:hi], in_=h_bf[:, PACK * lo:PACK * hi])
-            ybank = yps.tile([P, hi - lo], F32, name="ybank")
+        def layer2(lo, hi, codes):
+            nc.vector.quantize_mx(out=codes.bitcast(FP8X4), scales=h_sc[:, lo:hi], in_=h_bf[:, PACK * lo:PACK * hi])
+            ybank = banks.tile([P, hi - lo], F32, name="ybank", tag="bank")
             nc.tensor.matmul_mx(out=ybank[:], lhsT=w2_codes[:].bitcast(FP4X4), lhsT_scale=w2_sc[:],
-                                rhs=h_codes[:, lo:hi].bitcast(FP8X4), rhs_scale=h_sc[:, lo:hi], start=True, stop=True)
+                                rhs=codes.bitcast(FP8X4), rhs_scale=h_sc[:, lo:hi], start=True, stop=True)
             nc.scalar.activation(act[:, lo:hi], ybank[:], ACT.Gelu_apprx_tanh, bias=bias[:])
 
         def finish(lo, hi):
             nc.vector.tensor_tensor(fin[:, lo:hi], act[:, lo:hi], res[:, lo:hi], ADD)
             nc.sync.dma_start(out[:, lo:hi], fin[:, lo:hi])
 
-        for g in range(4):
-            gather_words(256 * g, 256 * (g + 1))
-            layer1(256 * g)
-            layer1(256 * g + CH)
-        for g in range(4):
-            layer2(256 * g, 256 * (g + 1))
-        for g in range(4):
-            gather_res(256 * g, 256 * (g + 1))
-        for g in range(4):
-            finish(256 * g, 256 * (g + 1))
+        for lo, hi in ((0, 256), (256, 512), (512, 1024)):
+            gather_words(lo, hi)
+            for c in range(lo, hi, CH):
+                layer1(c)
+        groups = ((0, 256), (256, 512), (512, 768), (768, 1024))
+        gather_res(0, S)
+        h_codes = keep.tile([P, S], U32, name="h_codes", align_bytes=64)
+        for lo, hi in groups:
+            layer2(lo, hi, h_codes[:, lo:hi])
+        for lo, hi in groups:
+            finish(lo, hi)

@@ -70,9 +70,9 @@ def tile_list_tabres_gelu_kernel(tc, tab_words, tab_scales, w1, w2_words, w2_sca
 
         nc.vector.tensor_copy(x_sc[:], scales_win[:].bitcast(U8).indirect(offsets[:]))
 
-        w1_view = w1_bf[:].rearrange("p (t m j) -> p m t j", t=PACK, j=PACK)
+        w1_view = w1_bf[:].rearrange("p (t m j) -> p m j t", t=PACK, j=PACK)
         for u in range(2):
-            nc.scalar.copy(w1_view[:, u * 64:(u + 1) * 64], w1_raw[u][:].rearrange("p j (m t) -> p m t j", t=PACK))
+            nc.scalar.copy(w1_view[:, u * 64:(u + 1) * 64], w1_raw[u][:].rearrange("p j (m t) -> p m j t", t=PACK))
         nc.vector.quantize_mx(out=w1_codes[:].bitcast(FP8X4), scales=w1_sc[:], in_=w1_bf[:])
 
         def gather_words(lo, hi):
@@ -104,7 +104,7 @@ def tile_list_tabres_gelu_kernel(tc, tab_words, tab_scales, w1, w2_words, w2_sca
             gather_words(lo, hi)
             for c in range(lo, hi, CH):
                 layer1(c)
-        groups = ((0, 256), (256, 512), (512, 768), (768, 1024))
+        groups = ((0, 256), (256, 512), (512, 768), (768, 896), (896, 1024))
         gather_res(0, S)
         h_codes = keep.tile([P, S], U32, name="h_codes", align_bytes=64)
         for lo, hi in groups:

@@ -19,7 +19,7 @@ ADD = mybir.AluOpType.add
 P = 128
 PACK = 4
 CH = 128
-GROUPS = [256,256,256,256]
+W1_PARTS = ((0, 288), (288, 512))
 
 
 def tile_list_tabres_gelu_kernel(tc, tab_words, tab_scales, w1, w2_words, w2_scales, rT, b, offs, out):
@@ -32,7 +32,7 @@ def tile_list_tabres_gelu_kernel(tc, tab_words, tab_scales, w1, w2_words, w2_sca
         words_win = keep.tile([P, T], I32, name="words_win", align_bytes=64)
         scales_win = keep.tile([P, T // 4], I32, name="scales_win", align_bytes=64)
         res_win = keep.tile([P, T], F32, name="res_win", align_bytes=64)
-        w1_raw = [keep.tile([P, PACK, H // 2], F32, name=f"w1_raw{u}") for u in range(2)]
+        w1_raw = [keep.tile([P, PACK, hi - lo], F32, name=f"w1_raw{lo}") for lo, hi in W1_PARTS]
         w1_bf = keep.tile([P, PACK * H], BF16, name="w1_bf", align_bytes=64)
         w1_codes = keep.tile([P, H], U32, name="w1_codes", align_bytes=64)
         w1_sc = keep.tile([P, H], U8, name="w1_sc", align_bytes=64)
@@ -54,12 +54,12 @@ def tile_list_tabres_gelu_kernel(tc, tab_words, tab_scales, w1, w2_words, w2_sca
         nc.gpsimd.memset(w2_sc[:], 0)
         nc.scalar.activation(warm2[:], warm[:], ACT.Gelu_apprx_tanh)
 
+        w1_rows = w1.rearrange("(p j) c -> p j c", j=PACK)
+        nc.sync.dma_start(w1_raw[0][:], w1_rows[:, :, slice(*W1_PARTS[0])])
         nc.sync.dma_start(offsets[:], offs)
         for r in range(4):
             nc.sync.dma_start(scales_win[r:P:32, :], tab_scales[0, r:16:4, :].bitcast(I32))
-        w1_rows = w1.rearrange("(p j) c -> p j c", j=PACK)
-        for u in range(2):
-            nc.sync.dma_start(w1_raw[u][:], w1_rows[:, :, u * (H // 2):(u + 1) * (H // 2)])
+        nc.sync.dma_start(w1_raw[1][:], w1_rows[:, :, slice(*W1_PARTS[1])])
         nc.sync.dma_start(words_win[:], tab_words[0].rearrange("p t i -> p (t i)").bitcast(I32))
         nc.sync.dma_start(res_win[:], rT)
         nc.sync.dma_start(w2_codes[:].bitcast(I32), w2_words[0].bitcast(I32))
@@ -71,8 +71,8 @@ def tile_list_tabres_gelu_kernel(tc, tab_words, tab_scales, w1, w2_words, w2_sca
         nc.vector.tensor_copy(x_sc[:], scales_win[:].bitcast(U8).indirect(offsets[:]))
 
         w1_view = w1_bf[:].rearrange("p (t m j) -> p m j t", t=PACK, j=PACK)
-        for u in range(2):
-            nc.scalar.copy(w1_view[:, u * 64:(u + 1) * 64], w1_raw[u][:].rearrange("p j (m t) -> p m j t", t=PACK))
+        for raw, (lo, hi) in zip(w1_raw, W1_PARTS):
+            nc.scalar.copy(w1_view[:, lo // PACK:hi // PACK], raw[:].rearrange("p j (m t) -> p m j t", t=PACK))
         nc.vector.quantize_mx(out=w1_codes[:].bitcast(FP8X4), scales=w1_sc[:], in_=w1_bf[:])
 
         def gather_words(lo, hi):

@@ -50,8 +50,8 @@ def tile_list_tabres_gelu_kernel(tc, tab_words, tab_scales, w1, w2_words, w2_sca
         fin = keep.tile([P, S], F32, name="fin", align_bytes=64)
 
         nc.vector.memset(scales_win[:], 0)
-        nc.gpsimd.memset(warm[:], 0.0)
-        nc.gpsimd.memset(w2_sc[:], 0)
+        nc.vector.memset(warm[:], 0.0)
+        nc.vector.memset(w2_sc[:].bitcast(I32), 0)
         nc.scalar.activation(warm2[:], warm[:], ACT.Gelu_apprx_tanh)
 
         w1_rows = w1.rearrange("(p j) c -> p j c", j=PACK)

@@ -19,7 +19,7 @@ ADD = mybir.AluOpType.add
 P = 128
 PACK = 4
 CH = 128
-W1_PARTS = ((0, 288), (288, 512))
+W1_PARTS = ((0, 224), (224, 512))
 
 
 def tile_list_tabres_gelu_kernel(tc, tab_words, tab_scales, w1, w2_words, w2_scales, rT, b, offs, out):
@@ -71,9 +71,14 @@ def tile_list_tabres_gelu_kernel(tc, tab_words, tab_scales, w1, w2_words, w2_sca
         nc.vector.tensor_copy(x_sc[:], scales_win[:].bitcast(U8).indirect(offsets[:]))
 
         w1_view = w1_bf[:].rearrange("p (t m j) -> p m j t", t=PACK, j=PACK)
-        for raw, (lo, hi) in zip(w1_raw, W1_PARTS):
-            nc.scalar.copy(w1_view[:, lo // PACK:hi // PACK], raw[:].rearrange("p j (m t) -> p m j t", t=PACK))
-        nc.vector.quantize_mx(out=w1_codes[:].bitcast(FP8X4), scales=w1_sc[:], in_=w1_bf[:])
+        w1_src = [raw[:].rearrange("p j (m t) -> p m j t", t=PACK) for raw in w1_raw]
+        cut = W1_PARTS[0][1] // PACK
+        nc.scalar.copy(w1_view[:, :cut], w1_src[0])
+        for u in range(2):
+            nc.scalar.copy(w1_view[:, cut:, :, 2 * u:2 * u + 2], w1_src[1][:, :, :, 2 * u:2 * u + 2])
+        for u in range(2):
+            cols = slice(u * 2 * P, (u + 1) * 2 * P)
+            nc.vector.quantize_mx(out=w1_codes[:, cols].bitcast(FP8X4), scales=w1_sc[:, cols], in_=w1_bf[:, u * 2 * H:(u + 1) * 2 * H])
 
         def gather_words(lo, hi):
             nc.vector.tensor_copy(x_codes[:, lo:hi], words_win[:].bitcast(U32).indirect(offsets[:, lo // 16:hi // 16]))

@@ -19,7 +19,7 @@ ADD = mybir.AluOpType.add
 P = 128
 PACK = 4
 CH = 128
-W1_PARTS = ((0, 224), (224, 512))
+W1_PARTS = ((0, 128), (128, 512))
 
 
 def tile_list_tabres_gelu_kernel(tc, tab_words, tab_scales, w1, w2_words, w2_scales, rT, b, offs, out):
@@ -74,8 +74,8 @@ def tile_list_tabres_gelu_kernel(tc, tab_words, tab_scales, w1, w2_words, w2_sca
         w1_src = [raw[:].rearrange("p j (m t) -> p m j t", t=PACK) for raw in w1_raw]
         cut = W1_PARTS[0][1] // PACK
         nc.scalar.copy(w1_view[:, :cut], w1_src[0])
-        for u in range(2):
-            nc.scalar.copy(w1_view[:, cut:, :, 2 * u:2 * u + 2], w1_src[1][:, :, :, 2 * u:2 * u + 2])
+        nc.scalar.copy(w1_view[:, cut:, :, 0:2], w1_src[1][:, :, :, 0:2])
+        nc.vector.tensor_copy(w1_view[:, cut:, :, 2:4], w1_src[1][:, :, :, 2:4])
         for u in range(2):
             cols = slice(u * 2 * P, (u + 1) * 2 * P)
             nc.vector.quantize_mx(out=w1_codes[:, cols].bitcast(FP8X4), scales=w1_sc[:, cols], in_=w1_bf[:, u * 2 * H:(u + 1) * 2 * H])

@@ -18,101 +18,111 @@ ADD = mybir.AluOpType.add
 
 P = 128
 PACK = 4
-CH = 128
-W1_PARTS = ((0, 128), (128, 512))
+GROUP = 16
+CHUNK = 128
+SPAN = 256
+W1_HEAD = 128
+WORD_GATHERS = ((0, 256), (256, 512), (512, 1024))
+LAYER2 = ((0, 512, 7), (512, 768, 0), (768, 1024, 1))
+LAST_CHUNK_BANK = LAYER2[0][1] // CHUNK - 1
 
 
 def tile_list_tabres_gelu_kernel(tc, tab_words, tab_scales, w1, w2_words, w2_scales, rT, b, offs, out):
     nc = tc.nc
     with ExitStack() as ctx:
         keep = ctx.enter_context(tc.tile_pool(name="keep", bufs=1))
-        banks = ctx.enter_context(tc.psum_pool(name="banks", bufs=8))
+        banks = ctx.enter_context(tc.psum_pool(name="banks", bufs=1))
 
-        offsets = keep.tile([P, S // 16], U16, name="offsets")
-        words_win = keep.tile([P, T], I32, name="words_win", align_bytes=64)
-        scales_win = keep.tile([P, T // 4], I32, name="scales_win", align_bytes=64)
-        res_win = keep.tile([P, T], F32, name="res_win", align_bytes=64)
-        w1_raw = [keep.tile([P, PACK, hi - lo], F32, name=f"w1_raw{lo}") for lo, hi in W1_PARTS]
+        offsets = keep.tile([P, S // GROUP], U16, name="offsets")
+        tab_words_sb = keep.tile([P, T], I32, name="tab_words_sb", align_bytes=64)
+        tab_scales_sb = keep.tile([P, T // 4], I32, name="tab_scales_sb", align_bytes=64)
+        rT_sb = keep.tile([P, T], F32, name="rT_sb", align_bytes=64)
+        w1_head = keep.tile([P, PACK, W1_HEAD], F32, name="w1_head")
+        w1_rest = keep.tile([P, PACK, H - W1_HEAD], F32, name="w1_rest")
         w1_bf = keep.tile([P, PACK * H], BF16, name="w1_bf", align_bytes=64)
         w1_codes = keep.tile([P, H], U32, name="w1_codes", align_bytes=64)
         w1_sc = keep.tile([P, H], U8, name="w1_sc", align_bytes=64)
         w2_codes = keep.tile([P, 2 * M], U8, name="w2_codes", align_bytes=64)
         w2_sc = keep.tile([P, M], U8, name="w2_sc", align_bytes=64)
         bias = keep.tile([P, 1], F32, name="bias")
-        warm = keep.tile([P, 1], F32, name="warm")
-        warm2 = keep.tile([P, 1], F32, name="warm2")
+        zero = keep.tile([P, 1], F32, name="zero")
+        relu_bias = keep.tile([P, 1], F32, name="relu_bias")
         x_codes = keep.tile([P, S], U32, name="x_codes", align_bytes=64)
         x_sc = keep.tile([P, S], U8, name="x_sc", align_bytes=64)
         h_bf = keep.tile([P, PACK * S], BF16, name="h_bf", align_bytes=64)
+        h_codes = keep.tile([P, S], U32, name="h_codes", align_bytes=64)
         h_sc = keep.tile([P, S], U8, name="h_sc", align_bytes=64)
-        res = keep.tile([P, S], F32, name="res", align_bytes=64)
+        res = keep.tile([P, S - SPAN], F32, name="res", align_bytes=64)
         act = keep.tile([P, S], F32, name="act", align_bytes=64)
         fin = keep.tile([P, S], F32, name="fin", align_bytes=64)
 
-        nc.vector.memset(scales_win[:], 0)
-        nc.vector.memset(warm[:], 0.0)
+        def entries(lo, hi):
+            return offsets[:, lo // GROUP:hi // GROUP]
+
+        nc.vector.memset(tab_scales_sb[:], 0)
+        nc.vector.memset(zero[:], 0.0)
         nc.vector.memset(w2_sc[:].bitcast(I32), 0)
-        nc.scalar.activation(warm2[:], warm[:], ACT.Gelu_apprx_tanh)
+        nc.scalar.activation(relu_bias[:], zero[:], ACT.Gelu_apprx_tanh)
 
         w1_rows = w1.rearrange("(p j) c -> p j c", j=PACK)
-        nc.sync.dma_start(w1_raw[0][:], w1_rows[:, :, slice(*W1_PARTS[0])])
+        nc.sync.dma_start(w1_head[:], w1_rows[:, :, :W1_HEAD])
         nc.sync.dma_start(offsets[:], offs)
         for r in range(4):
-            nc.sync.dma_start(scales_win[r:P:32, :], tab_scales[0, r:16:4, :].bitcast(I32))
-        nc.sync.dma_start(w1_raw[1][:], w1_rows[:, :, slice(*W1_PARTS[1])])
-        nc.sync.dma_start(words_win[:], tab_words[0].rearrange("p t i -> p (t i)").bitcast(I32))
-        nc.sync.dma_start(res_win[:], rT)
+            nc.sync.dma_start(tab_scales_sb[r:P:32, :], tab_scales[0, r:16:4, :].bitcast(I32))
+        nc.sync.dma_start(w1_rest[:], w1_rows[:, :, W1_HEAD:])
+        nc.sync.dma_start(tab_words_sb[:], tab_words[0].rearrange("p t i -> p (t i)").bitcast(I32))
+        nc.sync.dma_start(rT_sb[:], rT)
         nc.sync.dma_start(w2_codes[:].bitcast(I32), w2_words[0].bitcast(I32))
         with nc.allow_non_contiguous_dma(reason="one bias value a partition"):
             nc.sync.dma_start(bias[:], b.rearrange("(p o) -> p o", o=1))
         for r in range(4):
             nc.sync.dma_start(w2_sc[:].bitcast(I32)[r:P:32, :], w2_scales[0, r:16:4, :].bitcast(I32))
 
-        nc.vector.tensor_copy(x_sc[:], scales_win[:].bitcast(U8).indirect(offsets[:]))
+        nc.vector.tensor_copy(x_sc[:], tab_scales_sb[:].bitcast(U8).indirect(entries(0, S)))
 
-        w1_view = w1_bf[:].rearrange("p (t m j) -> p m j t", t=PACK, j=PACK)
-        w1_src = [raw[:].rearrange("p j (m t) -> p m j t", t=PACK) for raw in w1_raw]
-        cut = W1_PARTS[0][1] // PACK
-        nc.scalar.copy(w1_view[:, :cut], w1_src[0])
-        nc.scalar.copy(w1_view[:, cut:, :, 0:2], w1_src[1][:, :, :, 0:2])
-        nc.vector.tensor_copy(w1_view[:, cut:, :, 2:4], w1_src[1][:, :, :, 2:4])
-        for u in range(2):
-            cols = slice(u * 2 * P, (u + 1) * 2 * P)
-            nc.vector.quantize_mx(out=w1_codes[:, cols].bitcast(FP8X4), scales=w1_sc[:, cols], in_=w1_bf[:, u * 2 * H:(u + 1) * 2 * H])
-
-        def gather_words(lo, hi):
-            nc.vector.tensor_copy(x_codes[:, lo:hi], words_win[:].bitcast(U32).indirect(offsets[:, lo // 16:hi // 16]))
-
-        def gather_res(lo, hi):
-            nc.vector.tensor_copy(res[:, lo:hi], res_win[:].indirect(offsets[:, lo // 16:hi // 16]))
+        w1_dst = w1_bf[:].rearrange("p (t m j) -> p m j t", t=PACK, j=PACK)
+        head_src = w1_head[:].rearrange("p j (m t) -> p m j t", t=PACK)
+        rest_src = w1_rest[:].rearrange("p j (m t) -> p m j t", t=PACK)
+        m_head = W1_HEAD // PACK
+        nc.scalar.copy(w1_dst[:, :m_head], head_src)
+        nc.scalar.copy(w1_dst[:, m_head:, :, 0:2], rest_src[:, :, :, 0:2])
+        nc.vector.tensor_copy(w1_dst[:, m_head:, :, 2:4], rest_src[:, :, :, 2:4])
+        for lo in range(0, H, 2 * P):
+            hi = lo + 2 * P
+            nc.vector.quantize_mx(out=w1_codes[:, lo:hi].bitcast(FP8X4), scales=w1_sc[:, lo:hi], in_=w1_bf[:, PACK * lo:PACK * hi])
 
         def layer1(lo):
-            bank = banks.tile([P, PACK, CH], F32, name="hbank", tag="bank")
+            last = lo == S - CHUNK
+            bank = banks.tile([P, PACK, CHUNK], F32, name="hbank", tag=f"bank{LAST_CHUNK_BANK if last else lo // CHUNK}")
             for t in range(PACK):
                 nc.tensor.matmul_mx(out=bank[:, t, :], lhsT=w1_codes[:, t * P:(t + 1) * P].bitcast(FP8X4), lhsT_scale=w1_sc[:, t * P:(t + 1) * P],
-                                    rhs=x_codes[:, lo:lo + CH].bitcast(FP8X4), rhs_scale=x_sc[:, lo:lo + CH], start=True, stop=True)
-            nc.scalar.activation(h_bf[:, PACK * lo:PACK * (lo + CH)].rearrange("p (n t) -> p n t", t=PACK),
-                                 bank[:].rearrange("p t n -> p n t"), ACT.Relu)
+                                    rhs=x_codes[:, lo:lo + CHUNK].bitcast(FP8X4), rhs_scale=x_sc[:, lo:lo + CHUNK], start=True, stop=True)
+            dst = h_bf[:, PACK * lo:PACK * (lo + CHUNK)].rearrange("p (n t) -> p n t", t=PACK)
+            src = bank[:].rearrange("p t n -> p n t")
+            if last:
+                nc.vector.tensor_scalar_max(dst, src, 0.0)
+            else:
+                nc.scalar.activation(dst, src, ACT.Relu, bias=relu_bias[:])
 
-        def layer2(lo, hi, codes):
-            nc.vector.quantize_mx(out=codes.bitcast(FP8X4), scales=h_sc[:, lo:hi], in_=h_bf[:, PACK * lo:PACK * hi])
-            ybank = banks.tile([P, hi - lo], F32, name="ybank", tag="bank")
+        for lo, hi in WORD_GATHERS:
+            nc.vector.tensor_copy(x_codes[:, lo:hi], tab_words_sb[:].bitcast(U32).indirect(entries(lo, hi)))
+            for chunk_lo in range(lo, hi, CHUNK):
+                layer1(chunk_lo)
+
+        nc.vector.tensor_copy(res[:], rT_sb[:].indirect(entries(SPAN, S)))
+
+        for lo, hi, bank_no in LAYER2:
+            codes = h_codes[:, lo:hi].bitcast(FP8X4)
+            nc.vector.quantize_mx(out=codes, scales=h_sc[:, lo:hi], in_=h_bf[:, PACK * lo:PACK * hi])
+            ybank = banks.tile([P, hi - lo], F32, name="ybank", tag=f"bank{bank_no}")
             nc.tensor.matmul_mx(out=ybank[:], lhsT=w2_codes[:].bitcast(FP4X4), lhsT_scale=w2_sc[:],
-                                rhs=codes.bitcast(FP8X4), rhs_scale=h_sc[:, lo:hi], start=True, stop=True)
-            nc.scalar.activation(act[:, lo:hi], ybank[:], ACT.Gelu_apprx_tanh, bias=bias[:])
+                                rhs=codes, rhs_scale=h_sc[:, lo:hi], start=True, stop=True)
+            for at in range(0, hi - lo, SPAN):
+                nc.scalar.activation(act[:, lo + at:lo + at + SPAN], ybank[:, at:at + SPAN], ACT.Gelu_apprx_tanh, bias=bias[:])
 
-        def finish(lo, hi):
-            nc.vector.tensor_tensor(fin[:, lo:hi], act[:, lo:hi], res[:, lo:hi], ADD)
+        nc.vector.tensor_tensor(fin[:, :SPAN], rT_sb[:].indirect(entries(0, SPAN)), act[:, :SPAN], ADD)
+        nc.sync.dma_start(out[:, :SPAN], fin[:, :SPAN])
+        for lo in range(SPAN, S, SPAN):
+            hi = lo + SPAN
+            nc.vector.tensor_tensor(fin[:, lo:hi], act[:, lo:hi], res[:, lo - SPAN:hi - SPAN], ADD)
             nc.sync.dma_start(out[:, lo:hi], fin[:, lo:hi])
-
-        for lo, hi in ((0, 256), (256, 512), (512, 1024)):
-            gather_words(lo, hi)
-            for c in range(lo, hi, CH):
-                layer1(c)
-        groups = ((0, 256), (256, 512), (512, 768), (768, 896), (896, 1024))
-        gather_res(0, S)
-        h_codes = keep.tile([P, S], U32, name="h_codes", align_bytes=64)
-        for lo, hi in groups:
-            layer2(lo, hi, h_codes[:, lo:hi])
-        for lo, hi in groups:
-            finish(lo, hi)

@@ -20,7 +20,8 @@ P = 128
 PACK = 4
 GROUP = 16
 CHUNK = 128
-SPAN = 256
+SPANS = ((0, 256), (256, 512), (512, 768), (768, 896), (896, 1024))
+FUSED_FROM = 768
 W1_HEAD = 128
 WORD_GATHERS = ((0, 256), (256, 512), (512, 1024))
 LAYER2 = ((0, 512, 7), (512, 768, 0), (768, 1024, 1))
@@ -52,7 +53,7 @@ def tile_list_tabres_gelu_kernel(tc, tab_words, tab_scales, w1, w2_words, w2_sca
         h_bf = keep.tile([P, PACK * S], BF16, name="h_bf", align_bytes=64)
         h_codes = keep.tile([P, S], U32, name="h_codes", align_bytes=64)
         h_sc = keep.tile([P, S], U8, name="h_sc", align_bytes=64)
-        res = keep.tile([P, S - SPAN], F32, name="res", align_bytes=64)
+        res = keep.tile([P, FUSED_FROM], F32, name="res", align_bytes=64)
         act = keep.tile([P, S], F32, name="act", align_bytes=64)
         fin = keep.tile([P, S], F32, name="fin", align_bytes=64)
 
@@ -109,7 +110,7 @@ def tile_list_tabres_gelu_kernel(tc, tab_words, tab_scales, w1, w2_words, w2_sca
             for chunk_lo in range(lo, hi, CHUNK):
                 layer1(chunk_lo)
 
-        nc.vector.tensor_copy(res[:], rT_sb[:].indirect(entries(SPAN, S)))
+        nc.vector.tensor_copy(res[:], rT_sb[:].indirect(entries(0, FUSED_FROM)))
 
         for lo, hi, bank_no in LAYER2:
             codes = h_codes[:, lo:hi].bitcast(FP8X4)
@@ -117,12 +118,13 @@ def tile_list_tabres_gelu_kernel(tc, tab_words, tab_scales, w1, w2_words, w2_sca
             ybank = banks.tile([P, hi - lo], F32, name="ybank", tag=f"bank{bank_no}")
             nc.tensor.matmul_mx(out=ybank[:], lhsT=w2_codes[:].bitcast(FP4X4), lhsT_scale=w2_sc[:],
                                 rhs=codes, rhs_scale=h_sc[:, lo:hi], start=True, stop=True)
-            for at in range(0, hi - lo, SPAN):
-                nc.scalar.activation(act[:, lo + at:lo + at + SPAN], ybank[:, at:at + SPAN], ACT.Gelu_apprx_tanh, bias=bias[:])
+            for first, end in SPANS:
+                if lo <= first < hi:
+                    nc.scalar.activation(act[:, first:end], ybank[:, first - lo:end - lo], ACT.Gelu_apprx_tanh, bias=bias[:])
 
-        nc.vector.tensor_tensor(fin[:, :SPAN], rT_sb[:].indirect(entries(0, SPAN)), act[:, :SPAN], ADD)
-        nc.sync.dma_start(out[:, :SPAN], fin[:, :SPAN])
-        for lo in range(SPAN, S, SPAN):
-            hi = lo + SPAN
-            nc.vector.tensor_tensor(fin[:, lo:hi], act[:, lo:hi], res[:, lo - SPAN:hi - SPAN], ADD)
+        for lo, hi in SPANS:
+            if lo >= FUSED_FROM:
+                nc.vector.tensor_tensor(fin[:, lo:hi], rT_sb[:].indirect(entries(lo, hi)), act[:, lo:hi], ADD)
+            else:
+                nc.vector.tensor_tensor(fin[:, lo:hi], act[:, lo:hi], res[:, lo:hi], ADD)
             nc.sync.dma_start(out[:, lo:hi], fin[:, lo:hi])

@@ -22,7 +22,7 @@ GROUP = 16
 CHUNK = 128
 SPANS = ((0, 256), (256, 512), (512, 768), (768, 896), (896, 1024))
 FUSED_FROM = 768
-W1_HEAD = 128
+ROWS_AT = P - 16
 WORD_GATHERS = ((0, 256), (256, 512), (512, 1024))
 LAYER2 = ((0, 512, 7), (512, 768, 0), (768, 1024, 1))
 LAST_CHUNK_BANK = LAYER2[0][1] // CHUNK - 1
@@ -32,23 +32,19 @@ def tile_list_tabres_gelu_kernel(tc, tab_words, tab_scales, w1, w2_words, w2_sca
     nc = tc.nc
     with ExitStack() as ctx:
         keep = ctx.enter_context(tc.tile_pool(name="keep", bufs=1))
+        late = ctx.enter_context(tc.tile_pool(name="late", bufs=1))
         banks = ctx.enter_context(tc.psum_pool(name="banks", bufs=1))
 
         offsets = keep.tile([P, S // GROUP], U16, name="offsets")
         tab_words_sb = keep.tile([P, T], I32, name="tab_words_sb", align_bytes=64)
-        tab_scales_sb = keep.tile([P, T // 4], I32, name="tab_scales_sb", align_bytes=64)
-        rT_sb = keep.tile([P, T], F32, name="rT_sb", align_bytes=64)
-        w1_head = keep.tile([P, PACK, W1_HEAD], F32, name="w1_head")
-        w1_rest = keep.tile([P, PACK, H - W1_HEAD], F32, name="w1_rest")
+        w1_raw = keep.tile([P, PACK, H], F32, name="w1_raw")
         w1_bf = keep.tile([P, PACK * H], BF16, name="w1_bf", align_bytes=64)
         w1_codes = keep.tile([P, H], U32, name="w1_codes", align_bytes=64)
         w1_sc = keep.tile([P, H], U8, name="w1_sc", align_bytes=64)
-        w2_codes = keep.tile([P, 2 * M], U8, name="w2_codes", align_bytes=64)
-        w2_sc = keep.tile([P, M], U8, name="w2_sc", align_bytes=64)
-        bias = keep.tile([P, 1], F32, name="bias")
         zero = keep.tile([P, 1], F32, name="zero")
         relu_bias = keep.tile([P, 1], F32, name="relu_bias")
         x_codes = keep.tile([P, S], U32, name="x_codes", align_bytes=64)
+        x_sc_rows = keep.tile([P, S], U8, name="x_sc_rows", align_bytes=64)
         x_sc = keep.tile([P, S], U8, name="x_sc", align_bytes=64)
         h_bf = keep.tile([P, PACK * S], BF16, name="h_bf", align_bytes=64)
         h_codes = keep.tile([P, S], U32, name="h_codes", align_bytes=64)
@@ -56,22 +52,30 @@ def tile_list_tabres_gelu_kernel(tc, tab_words, tab_scales, w1, w2_words, w2_sca
         res = keep.tile([P, FUSED_FROM], F32, name="res", align_bytes=64)
         act = keep.tile([P, S], F32, name="act", align_bytes=64)
         fin = keep.tile([P, S], F32, name="fin", align_bytes=64)
+        tab_scales_sb = late.tile([P, T // 4], I32, name="tab_scales_sb", align_bytes=64, offset=4 * T - T // 2)
+        rT_sb = late.tile([P, T], F32, name="rT_sb", align_bytes=64, offset=0)
+        w2_codes = late.tile([P, 2 * M], U8, name="w2_codes", align_bytes=64, offset=4 * T)
+        w2_sc = late.tile([P, M], U8, name="w2_sc", align_bytes=64, offset=4 * T + 2 * M)
+        bias = late.tile([P, 1], F32, name="bias", align_bytes=64, offset=4 * T + 3 * M)
 
         def entries(lo, hi):
             return offsets[:, lo // GROUP:hi // GROUP]
 
-        nc.vector.memset(tab_scales_sb[:], 0)
+        nc.vector.memset(tab_scales_sb[:ROWS_AT, :], 0)
         nc.vector.memset(zero[:], 0.0)
-        nc.vector.memset(w2_sc[:].bitcast(I32), 0)
+        nc.vector.memset(x_sc[:].bitcast(I32), 0)
         nc.scalar.activation(relu_bias[:], zero[:], ACT.Gelu_apprx_tanh)
 
-        w1_rows = w1.rearrange("(p j) c -> p j c", j=PACK)
-        nc.sync.dma_start(w1_head[:], w1_rows[:, :, :W1_HEAD])
+        nc.sync.dma_start(tab_scales_sb[ROWS_AT:ROWS_AT + 16, :], tab_scales[0].bitcast(I32))
         nc.sync.dma_start(offsets[:], offs)
-        for r in range(4):
-            nc.sync.dma_start(tab_scales_sb[r:P:32, :], tab_scales[0, r:16:4, :].bitcast(I32))
-        nc.sync.dma_start(w1_rest[:], w1_rows[:, :, W1_HEAD:])
+        nc.sync.dma_start(w1_raw[:], w1.rearrange("(p j) c -> p j c", j=PACK))
         nc.sync.dma_start(tab_words_sb[:], tab_words[0].rearrange("p t i -> p (t i)").bitcast(I32))
+
+        nc.vector.tensor_copy(x_sc_rows[:], tab_scales_sb[:].bitcast(U8).indirect(entries(0, S)))
+        for q in range(4):
+            nc.sync.dma_start(x_sc[:].bitcast(I32)[32 * q:32 * q + 4, :], x_sc_rows[:].bitcast(I32)[ROWS_AT + 4 * q:ROWS_AT + 4 * q + 4, :])
+
+        nc.vector.memset(w2_sc[:].bitcast(I32), 0)
         nc.sync.dma_start(rT_sb[:], rT)
         nc.sync.dma_start(w2_codes[:].bitcast(I32), w2_words[0].bitcast(I32))
         with nc.allow_non_contiguous_dma(reason="one bias value a partition"):
@@ -79,15 +83,10 @@ def tile_list_tabres_gelu_kernel(tc, tab_words, tab_scales, w1, w2_words, w2_sca
         for r in range(4):
             nc.sync.dma_start(w2_sc[:].bitcast(I32)[r:P:32, :], w2_scales[0, r:16:4, :].bitcast(I32))
 
-        nc.vector.tensor_copy(x_sc[:], tab_scales_sb[:].bitcast(U8).indirect(entries(0, S)))
-
         w1_dst = w1_bf[:].rearrange("p (t m j) -> p m j t", t=PACK, j=PACK)
-        head_src = w1_head[:].rearrange("p j (m t) -> p m j t", t=PACK)
-        rest_src = w1_rest[:].rearrange("p j (m t) -> p m j t", t=PACK)
-        m_head = W1_HEAD // PACK
-        nc.scalar.copy(w1_dst[:, :m_head], head_src)
-        nc.scalar.copy(w1_dst[:, m_head:, :, 0:2], rest_src[:, :, :, 0:2])
-        nc.vector.tensor_copy(w1_dst[:, m_head:, :, 2:4], rest_src[:, :, :, 2:4])
+        w1_src = w1_raw[:].rearrange("p j (m t) -> p m j t", t=PACK)
+        nc.scalar.copy(w1_dst[:, :, :, 0:2], w1_src[:, :, :, 0:2])
+        nc.vector.tensor_copy(w1_dst[:, :, :, 2:4], w1_src[:, :, :, 2:4])
         for lo in range(0, H, 2 * P):
             hi = lo + 2 * P
             nc.vector.quantize_mx(out=w1_codes[:, lo:hi].bitcast(FP8X4), scales=w1_sc[:, lo:hi], in_=w1_bf[:, PACK * lo:PACK * hi])

@@ -23,6 +23,7 @@ CHUNK = 128
 SPANS = ((0, 256), (256, 512), (512, 768), (768, 896), (896, 1024))
 FUSED_FROM = 768
 ROWS_AT = P - 16
+SCALES_AHEAD = 512
 WORD_GATHERS = ((0, 256), (256, 512), (512, 1024))
 LAYER2 = ((0, 512, 7), (512, 768, 0), (768, 1024, 1))
 LAST_CHUNK_BANK = LAYER2[0][1] // CHUNK - 1
@@ -45,7 +46,9 @@ def tile_list_tabres_gelu_kernel(tc, tab_words, tab_scales, w1, w2_words, w2_sca
         relu_bias = keep.tile([P, 1], F32, name="relu_bias")
         x_codes = keep.tile([P, S], U32, name="x_codes", align_bytes=64)
         x_sc_rows = keep.tile([P, S], U8, name="x_sc_rows", align_bytes=64)
-        x_sc = keep.tile([P, S], U8, name="x_sc", align_bytes=64)
+        late_rows = keep.tile([P, S - SCALES_AHEAD + M], U8, name="late_rows", align_bytes=64)
+        planes = keep.tile([P, S + M], U8, name="planes", align_bytes=64)
+        x_sc, w2_sc = planes[:, :S], planes[:, S:]
         h_bf = keep.tile([P, PACK * S], BF16, name="h_bf", align_bytes=64)
         h_codes = keep.tile([P, S], U32, name="h_codes", align_bytes=64)
         h_sc = keep.tile([P, S], U8, name="h_sc", align_bytes=64)
@@ -55,15 +58,14 @@ def tile_list_tabres_gelu_kernel(tc, tab_words, tab_scales, w1, w2_words, w2_sca
         tab_scales_sb = late.tile([P, T // 4], I32, name="tab_scales_sb", align_bytes=64, offset=4 * T - T // 2)
         rT_sb = late.tile([P, T], F32, name="rT_sb", align_bytes=64, offset=0)
         w2_codes = late.tile([P, 2 * M], U8, name="w2_codes", align_bytes=64, offset=4 * T)
-        w2_sc = late.tile([P, M], U8, name="w2_sc", align_bytes=64, offset=4 * T + 2 * M)
-        bias = late.tile([P, 1], F32, name="bias", align_bytes=64, offset=4 * T + 3 * M)
+        bias = late.tile([P, 1], F32, name="bias", align_bytes=64, offset=4 * T + 2 * M)
 
         def entries(lo, hi):
             return offsets[:, lo // GROUP:hi // GROUP]
 
         nc.vector.memset(tab_scales_sb[:ROWS_AT, :], 0)
         nc.vector.memset(zero[:], 0.0)
-        nc.vector.memset(x_sc[:].bitcast(I32), 0)
+        nc.vector.memset(planes[:].bitcast(I32), 0)
         nc.scalar.activation(relu_bias[:], zero[:], ACT.Gelu_apprx_tanh)
 
         nc.sync.dma_start(tab_scales_sb[ROWS_AT:ROWS_AT + 16, :], tab_scales[0].bitcast(I32))
@@ -71,17 +73,22 @@ def tile_list_tabres_gelu_kernel(tc, tab_words, tab_scales, w1, w2_words, w2_sca
         nc.sync.dma_start(w1_raw[:], w1.rearrange("(p j) c -> p j c", j=PACK))
         nc.sync.dma_start(tab_words_sb[:], tab_words[0].rearrange("p t i -> p (t i)").bitcast(I32))
 
-        nc.vector.tensor_copy(x_sc_rows[:], tab_scales_sb[:].bitcast(U8).indirect(entries(0, S)))
-        for q in range(4):
-            nc.sync.dma_start(x_sc[:].bitcast(I32)[32 * q:32 * q + 4, :], x_sc_rows[:].bitcast(I32)[ROWS_AT + 4 * q:ROWS_AT + 4 * q + 4, :])
+        nc.sync.dma_start(late_rows[:].bitcast(I32)[ROWS_AT:, (S - SCALES_AHEAD) // 4:], w2_scales[0].bitcast(I32))
 
-        nc.vector.memset(w2_sc[:].bitcast(I32), 0)
+        def move_scales(dst, src):
+            for q in range(4):
+                nc.sync.dma_start(dst[32 * q:32 * q + 4, :], src[ROWS_AT + 4 * q:ROWS_AT + 4 * q + 4, :])
+
+        for lo, hi in ((0, SCALES_AHEAD), (SCALES_AHEAD, S)):
+            nc.vector.tensor_copy(x_sc_rows[:, lo:hi], tab_scales_sb[:].bitcast(U8).indirect(entries(lo, hi)))
+        ahead = SCALES_AHEAD // 4
+        move_scales(planes[:].bitcast(I32)[:, :ahead], x_sc_rows[:].bitcast(I32)[:, :ahead])
         nc.sync.dma_start(rT_sb[:], rT)
+        nc.vector.tensor_copy(late_rows[:].bitcast(I32)[:, :S // 4 - ahead], x_sc_rows[:].bitcast(I32)[:, ahead:])
+        move_scales(planes[:].bitcast(I32)[:, ahead:], late_rows[:].bitcast(I32))
         nc.sync.dma_start(w2_codes[:].bitcast(I32), w2_words[0].bitcast(I32))
         with nc.allow_non_contiguous_dma(reason="one bias value a partition"):
             nc.sync.dma_start(bias[:], b.rearrange("(p o) -> p o", o=1))
-        for r in range(4):
-            nc.sync.dma_start(w2_sc[:].bitcast(I32)[r:P:32, :], w2_scales[0, r:16:4, :].bitcast(I32))
 
         w1_dst = w1_bf[:].rearrange("p (t m j) -> p m j t", t=PACK, j=PACK)
         w1_src = w1_raw[:].rearrange("p j (m t) -> p m j t", t=PACK)
@@ -115,7 +122,7 @@ def tile_list_tabres_gelu_kernel(tc, tab_words, tab_scales, w1, w2_words, w2_sca
             codes = h_codes[:, lo:hi].bitcast(FP8X4)
             nc.vector.quantize_mx(out=codes, scales=h_sc[:, lo:hi], in_=h_bf[:, PACK * lo:PACK * hi])
             ybank = banks.tile([P, hi - lo], F32, name="ybank", tag=f"bank{bank_no}")
-            nc.tensor.matmul_mx(out=ybank[:], lhsT=w2_codes[:].bitcast(FP4X4), lhsT_scale=w2_sc[:],
+            nc.tensor.matmul_mx(out=ybank[:], lhsT=w2_codes[:].bitcast(FP4X4), lhsT_scale=w2_sc,
                                 rhs=codes, rhs_scale=h_sc[:, lo:hi], start=True, stop=True)
             for first, end in SPANS:
                 if lo <= first < hi:

@@ -46,9 +46,7 @@ def tile_list_tabres_gelu_kernel(tc, tab_words, tab_scales, w1, w2_words, w2_sca
         relu_bias = keep.tile([P, 1], F32, name="relu_bias")
         x_codes = keep.tile([P, S], U32, name="x_codes", align_bytes=64)
         x_sc_rows = keep.tile([P, S], U8, name="x_sc_rows", align_bytes=64)
-        late_rows = keep.tile([P, S - SCALES_AHEAD + M], U8, name="late_rows", align_bytes=64)
-        planes = keep.tile([P, S + M], U8, name="planes", align_bytes=64)
-        x_sc, w2_sc = planes[:, :S], planes[:, S:]
+        x_sc = keep.tile([P, S], U8, name="x_sc", align_bytes=64)
         h_bf = keep.tile([P, PACK * S], BF16, name="h_bf", align_bytes=64)
         h_codes = keep.tile([P, S], U32, name="h_codes", align_bytes=64)
         h_sc = keep.tile([P, S], U8, name="h_sc", align_bytes=64)
@@ -58,6 +56,7 @@ def tile_list_tabres_gelu_kernel(tc, tab_words, tab_scales, w1, w2_words, w2_sca
         tab_scales_sb = late.tile([P, T // 4], I32, name="tab_scales_sb", align_bytes=64, offset=4 * T - T // 2)
         rT_sb = late.tile([P, T], F32, name="rT_sb", align_bytes=64, offset=0)
         w2_codes = late.tile([P, 2 * M], U8, name="w2_codes", align_bytes=64, offset=4 * T)
+        w2_sc = late.tile([P, M], U8, name="w2_sc", align_bytes=64, offset=4 * T + 2 * M + 64)
         bias = late.tile([P, 1], F32, name="bias", align_bytes=64, offset=4 * T + 2 * M)
 
         def entries(lo, hi):
@@ -65,15 +64,13 @@ def tile_list_tabres_gelu_kernel(tc, tab_words, tab_scales, w1, w2_words, w2_sca
 
         nc.vector.memset(tab_scales_sb[:ROWS_AT, :], 0)
         nc.vector.memset(zero[:], 0.0)
-        nc.vector.memset(planes[:].bitcast(I32), 0)
+        nc.vector.memset(x_sc[:].bitcast(I32), 0)
         nc.scalar.activation(relu_bias[:], zero[:], ACT.Gelu_apprx_tanh)
 
-        nc.sync.dma_start(tab_scales_sb[ROWS_AT:ROWS_AT + 16, :], tab_scales[0].bitcast(I32))
+        nc.scalar.dma_start(tab_scales_sb[ROWS_AT:ROWS_AT + 16, :], tab_scales[0].bitcast(I32))
         nc.sync.dma_start(offsets[:], offs)
         nc.sync.dma_start(w1_raw[:], w1.rearrange("(p j) c -> p j c", j=PACK))
         nc.sync.dma_start(tab_words_sb[:], tab_words[0].rearrange("p t i -> p (t i)").bitcast(I32))
-
-        nc.sync.dma_start(late_rows[:].bitcast(I32)[ROWS_AT:, (S - SCALES_AHEAD) // 4:], w2_scales[0].bitcast(I32))
 
         def move_scales(dst, src):
             for q in range(4):
@@ -82,10 +79,12 @@ def tile_list_tabres_gelu_kernel(tc, tab_words, tab_scales, w1, w2_words, w2_sca
         for lo, hi in ((0, SCALES_AHEAD), (SCALES_AHEAD, S)):
             nc.vector.tensor_copy(x_sc_rows[:, lo:hi], tab_scales_sb[:].bitcast(U8).indirect(entries(lo, hi)))
         ahead = SCALES_AHEAD // 4
-        move_scales(planes[:].bitcast(I32)[:, :ahead], x_sc_rows[:].bitcast(I32)[:, :ahead])
+        move_scales(x_sc[:].bitcast(I32)[:, :ahead], x_sc_rows[:].bitcast(I32)[:, :ahead])
         nc.sync.dma_start(rT_sb[:], rT)
-        nc.vector.tensor_copy(late_rows[:].bitcast(I32)[:, :S // 4 - ahead], x_sc_rows[:].bitcast(I32)[:, ahead:])
-        move_scales(planes[:].bitcast(I32)[:, ahead:], late_rows[:].bitcast(I32))
+        move_scales(x_sc[:].bitcast(I32)[:, ahead:], x_sc_rows[:].bitcast(I32)[:, ahead:])
+        nc.vector.memset(w2_sc[:].bitcast(I32), 0)
+        for q in range(4):
+            nc.sync.dma_start(w2_sc[:].bitcast(I32)[32 * q:32 * q + 4, :], w2_scales[0].bitcast(I32)[4 * q:4 * q + 4, :])
         nc.sync.dma_start(w2_codes[:].bitcast(I32), w2_words[0].bitcast(I32))
         with nc.allow_non_contiguous_dma(reason="one bias value a partition"):
             nc.sync.dma_start(bias[:], b.rearrange("(p o) -> p o", o=1))
@@ -122,7 +121,7 @@ def tile_list_tabres_gelu_kernel(tc, tab_words, tab_scales, w1, w2_words, w2_sca
             codes = h_codes[:, lo:hi].bitcast(FP8X4)
             nc.vector.quantize_mx(out=codes, scales=h_sc[:, lo:hi], in_=h_bf[:, PACK * lo:PACK * hi])
             ybank = banks.tile([P, hi - lo], F32, name="ybank", tag=f"bank{bank_no}")
-            nc.tensor.matmul_mx(out=ybank[:], lhsT=w2_codes[:].bitcast(FP4X4), lhsT_scale=w2_sc,
+            nc.tensor.matmul_mx(out=ybank[:], lhsT=w2_codes[:].bitcast(FP4X4), lhsT_scale=w2_sc[:],
                                 rhs=codes, rhs_scale=h_sc[:, lo:hi], start=True, stop=True)
             for first, end in SPANS:
                 if lo <= first < hi:

@@ -20,13 +20,13 @@ P = 128
 PACK = 4
 GROUP = 16
 CHUNK = 128
-SPANS = ((0, 256), (256, 512), (512, 768), (768, 896), (896, 1024))
-FUSED_FROM = 768
 ROWS_AT = P - 16
-SCALES_AHEAD = 512
-WORD_GATHERS = ((0, 256), (256, 512), (512, 1024))
-LAYER2 = ((0, 512, 7), (512, 768, 0), (768, 1024, 1))
-LAST_CHUNK_BANK = LAYER2[0][1] // CHUNK - 1
+SCALES_AHEAD = 768
+WORD_GATHERS = ((0, 256), (256, 512), (512, 768), (768, 1024),)
+GROUPS = ((0, 256), (256, 512), (512, 768), (768, 896), (896, 1024),)
+SPANS = ((0, 256), (256, 512), (512, 768), (768, 896), (896, 1024),)
+VECTOR_RELUS = (3, 4)
+AHEAD = ((512, 768),)
 
 
 def tile_list_tabres_gelu_kernel(tc, tab_words, tab_scales, w1, w2_words, w2_scales, rT, b, offs, out):
@@ -46,17 +46,18 @@ def tile_list_tabres_gelu_kernel(tc, tab_words, tab_scales, w1, w2_words, w2_sca
         relu_bias = keep.tile([P, 1], F32, name="relu_bias")
         x_codes = keep.tile([P, S], U32, name="x_codes", align_bytes=64)
         x_sc_rows = keep.tile([P, S], U8, name="x_sc_rows", align_bytes=64)
-        x_sc = keep.tile([P, S], U8, name="x_sc", align_bytes=64)
+        staged = keep.tile([P, S - SCALES_AHEAD + M], U8, name="staged", align_bytes=64)
+        x_sc = keep.tile([P, S + M], U8, name="x_sc", align_bytes=64)
         h_bf = keep.tile([P, PACK * S], BF16, name="h_bf", align_bytes=64)
         h_codes = keep.tile([P, S], U32, name="h_codes", align_bytes=64)
         h_sc = keep.tile([P, S], U8, name="h_sc", align_bytes=64)
-        res = keep.tile([P, FUSED_FROM], F32, name="res", align_bytes=64)
+        res = keep.tile([P, S], F32, name="res", align_bytes=64)
         act = keep.tile([P, S], F32, name="act", align_bytes=64)
         fin = keep.tile([P, S], F32, name="fin", align_bytes=64)
+
         tab_scales_sb = late.tile([P, T // 4], I32, name="tab_scales_sb", align_bytes=64, offset=4 * T - T // 2)
         rT_sb = late.tile([P, T], F32, name="rT_sb", align_bytes=64, offset=0)
         w2_codes = late.tile([P, 2 * M], U8, name="w2_codes", align_bytes=64, offset=4 * T)
-        w2_sc = late.tile([P, M], U8, name="w2_sc", align_bytes=64, offset=4 * T + 2 * M + 64)
         bias = late.tile([P, 1], F32, name="bias", align_bytes=64, offset=4 * T + 2 * M)
 
         def entries(lo, hi):
@@ -67,27 +68,28 @@ def tile_list_tabres_gelu_kernel(tc, tab_words, tab_scales, w1, w2_words, w2_sca
         nc.vector.memset(x_sc[:].bitcast(I32), 0)
         nc.scalar.activation(relu_bias[:], zero[:], ACT.Gelu_apprx_tanh)
 
+        words = tab_words[0].rearrange("p t i -> p (t i)").bitcast(I32)
         nc.scalar.dma_start(tab_scales_sb[ROWS_AT:ROWS_AT + 16, :], tab_scales[0].bitcast(I32))
         nc.sync.dma_start(offsets[:], offs)
         nc.sync.dma_start(w1_raw[:], w1.rearrange("(p j) c -> p j c", j=PACK))
-        nc.sync.dma_start(tab_words_sb[:], tab_words[0].rearrange("p t i -> p (t i)").bitcast(I32))
+        nc.sync.dma_start(staged[:].bitcast(I32)[ROWS_AT:, (S - SCALES_AHEAD) // 4:], w2_scales[0].bitcast(I32))
+        nc.sync.dma_start(tab_words_sb[:, :512], words[:, :512])
+        nc.sync.dma_start(tab_words_sb[:, 512:], words[:, 512:])
 
         def move_scales(dst, src):
             for q in range(4):
                 nc.sync.dma_start(dst[32 * q:32 * q + 4, :], src[ROWS_AT + 4 * q:ROWS_AT + 4 * q + 4, :])
 
-        for lo, hi in ((0, SCALES_AHEAD), (SCALES_AHEAD, S)):
+        for lo, hi in ((0, 768), (768, S)):
             nc.vector.tensor_copy(x_sc_rows[:, lo:hi], tab_scales_sb[:].bitcast(U8).indirect(entries(lo, hi)))
         ahead = SCALES_AHEAD // 4
         move_scales(x_sc[:].bitcast(I32)[:, :ahead], x_sc_rows[:].bitcast(I32)[:, :ahead])
         nc.sync.dma_start(rT_sb[:], rT)
-        move_scales(x_sc[:].bitcast(I32)[:, ahead:], x_sc_rows[:].bitcast(I32)[:, ahead:])
-        nc.vector.memset(w2_sc[:].bitcast(I32), 0)
-        for q in range(4):
-            nc.sync.dma_start(w2_sc[:].bitcast(I32)[32 * q:32 * q + 4, :], w2_scales[0].bitcast(I32)[4 * q:4 * q + 4, :])
         nc.sync.dma_start(w2_codes[:].bitcast(I32), w2_words[0].bitcast(I32))
         with nc.allow_non_contiguous_dma(reason="one bias value a partition"):
             nc.sync.dma_start(bias[:], b.rearrange("(p o) -> p o", o=1))
+        nc.vector.tensor_copy(staged[:].bitcast(I32)[:, :S // 4 - ahead], x_sc_rows[:].bitcast(I32)[:, ahead:])
+        move_scales(x_sc[:].bitcast(I32)[:, ahead:], staged[:].bitcast(I32))
 
         w1_dst = w1_bf[:].rearrange("p (t m j) -> p m j t", t=PACK, j=PACK)
         w1_src = w1_raw[:].rearrange("p j (m t) -> p m j t", t=PACK)
@@ -97,39 +99,108 @@ def tile_list_tabres_gelu_kernel(tc, tab_words, tab_scales, w1, w2_words, w2_sca
             hi = lo + 2 * P
             nc.vector.quantize_mx(out=w1_codes[:, lo:hi].bitcast(FP8X4), scales=w1_sc[:, lo:hi], in_=w1_bf[:, PACK * lo:PACK * hi])
 
-        def layer1(lo):
-            last = lo == S - CHUNK
-            bank = banks.tile([P, PACK, CHUNK], F32, name="hbank", tag=f"bank{LAST_CHUNK_BANK if last else lo // CHUNK}")
+        hbanks = {}
+        ybanks = {}
+        warm = banks.tile([P, 512], F32, name="warm", tag="bank7")
+        for rep in range(3):
+            nc.tensor.matmul_mx(out=warm[:32, :], lhsT=tab_words_sb[:, :32].bitcast(FP8X4), lhsT_scale=x_sc_rows[:, :32],
+                                rhs=tab_words_sb[:, :512].bitcast(FP8X4), rhs_scale=x_sc_rows[:, :512], start=True, stop=True)
+
+        def g(lo):
+            hi = dict(WORD_GATHERS)[lo]
+            nc.vector.tensor_copy(x_codes[:, lo:hi], tab_words_sb[:].bitcast(U32).indirect(entries(lo, hi)))
+
+        def m(c, bank_no):
+            lo = c * CHUNK
+            bank = banks.tile([P, PACK, CHUNK], F32, name="hbank", tag=f"bank{bank_no}")
+            hbanks[c] = bank
             for t in range(PACK):
                 nc.tensor.matmul_mx(out=bank[:, t, :], lhsT=w1_codes[:, t * P:(t + 1) * P].bitcast(FP8X4), lhsT_scale=w1_sc[:, t * P:(t + 1) * P],
                                     rhs=x_codes[:, lo:lo + CHUNK].bitcast(FP8X4), rhs_scale=x_sc[:, lo:lo + CHUNK], start=True, stop=True)
+
+        def r(c):
+            lo = c * CHUNK
             dst = h_bf[:, PACK * lo:PACK * (lo + CHUNK)].rearrange("p (n t) -> p n t", t=PACK)
-            src = bank[:].rearrange("p t n -> p n t")
-            if last:
+            src = hbanks[c][:].rearrange("p t n -> p n t")
+            if c in VECTOR_RELUS:
                 nc.vector.tensor_scalar_max(dst, src, 0.0)
             else:
                 nc.scalar.activation(dst, src, ACT.Relu, bias=relu_bias[:])
 
-        for lo, hi in WORD_GATHERS:
-            nc.vector.tensor_copy(x_codes[:, lo:hi], tab_words_sb[:].bitcast(U32).indirect(entries(lo, hi)))
-            for chunk_lo in range(lo, hi, CHUNK):
-                layer1(chunk_lo)
+        def p(lo):
+            hi = dict(AHEAD)[lo]
+            nc.vector.tensor_copy(res[:, lo:hi], rT_sb[:].indirect(entries(lo, hi)))
 
-        nc.vector.tensor_copy(res[:], rT_sb[:].indirect(entries(0, FUSED_FROM)))
+        def q(lo):
+            hi = dict(GROUPS)[lo]
+            nc.vector.quantize_mx(out=h_codes[:, lo:hi].bitcast(FP8X4), scales=h_sc[:, lo:hi], in_=h_bf[:, PACK * lo:PACK * hi])
 
-        for lo, hi, bank_no in LAYER2:
+        def y(lo, bank_no):
+            hi = dict(GROUPS)[lo]
             codes = h_codes[:, lo:hi].bitcast(FP8X4)
-            nc.vector.quantize_mx(out=codes, scales=h_sc[:, lo:hi], in_=h_bf[:, PACK * lo:PACK * hi])
             ybank = banks.tile([P, hi - lo], F32, name="ybank", tag=f"bank{bank_no}")
-            nc.tensor.matmul_mx(out=ybank[:], lhsT=w2_codes[:].bitcast(FP4X4), lhsT_scale=w2_sc[:],
+            ybanks[lo] = ybank
+            nc.tensor.matmul_mx(out=ybank[:], lhsT=w2_codes[:].bitcast(FP4X4), lhsT_scale=x_sc[:, S:],
                                 rhs=codes, rhs_scale=h_sc[:, lo:hi], start=True, stop=True)
-            for first, end in SPANS:
-                if lo <= first < hi:
-                    nc.scalar.activation(act[:, first:end], ybank[:, first - lo:end - lo], ACT.Gelu_apprx_tanh, bias=bias[:])
 
-        for lo, hi in SPANS:
-            if lo >= FUSED_FROM:
-                nc.vector.tensor_tensor(fin[:, lo:hi], rT_sb[:].indirect(entries(lo, hi)), act[:, lo:hi], ADD)
-            else:
+        def e(lo):
+            hi = dict(SPANS)[lo]
+            first = max(a for a, z in GROUPS if a <= lo)
+            nc.scalar.activation(act[:, lo:hi], ybanks[first][:, lo - first:hi - first], ACT.Gelu_apprx_tanh, bias=bias[:])
+
+        def a(lo):
+            hi = dict(SPANS)[lo]
+            if any(x <= lo < z for x, z in AHEAD):
                 nc.vector.tensor_tensor(fin[:, lo:hi], act[:, lo:hi], res[:, lo:hi], ADD)
+            else:
+                nc.vector.tensor_tensor(fin[:, lo:hi], rT_sb[:].indirect(entries(lo, hi)), act[:, lo:hi], ADD)
+
+        def s(lo, hi):
             nc.sync.dma_start(out[:, lo:hi], fin[:, lo:hi])
+
+        g(0)
+        m(0, 0)
+        m(1, 1)
+        g(256)
+        m(2, 2)
+        m(3, 3)
+        g(512)
+        m(4, 4)
+        m(5, 5)
+        g(768)
+        m(6, 6)
+        r(0)
+        r(1)
+        r(2)
+        r(3)
+        p(512)
+        q(0)
+        y(0, 0)
+        m(7, 7)
+        r(4)
+        q(256)
+        y(256, 1)
+        r(5)
+        r(6)
+        e(0)
+        r(7)
+        q(512)
+        y(512, 2)
+        q(768)
+        y(768, 3)
+        a(0)
+        s(0, 256)
+        q(896)
+        y(896, 4)
+        e(256)
+        a(256)
+        s(256, 512)
+        e(512)
+        a(512)
+        s(512, 768)
+        e(768)
+        a(768)
+        s(768, 896)
+        e(896)
+        a(896)
+        s(896, 1024)

@@ -22,7 +22,7 @@ GROUP = 16
 CHUNK = 128
 ROWS_AT = P - 16
 SCALES_AHEAD = 768
-WORD_GATHERS = ((0, 256), (256, 512), (512, 768), (768, 1024),)
+WORD_GATHERS = ((0, 128), (128, 384), (384, 640), (640, 1024))
 GROUPS = ((0, 256), (256, 512), (512, 768), (768, 896), (896, 1024),)
 SPANS = ((0, 256), (256, 512), (512, 768), (768, 896), (896, 1024),)
 VECTOR_RELUS = (3, 4)
@@ -160,14 +160,14 @@ def tile_list_tabres_gelu_kernel(tc, tab_words, tab_scales, w1, w2_words, w2_sca
 
         g(0)
         m(0, 0)
+        g(128)
         m(1, 1)
-        g(256)
         m(2, 2)
+        g(384)
         m(3, 3)
-        g(512)
         m(4, 4)
+        g(640)
         m(5, 5)
-        g(768)
         m(6, 6)
         r(0)
         r(1)

@@ -25,8 +25,8 @@ SCALES_AHEAD = 768
 WORD_GATHERS = ((0, 128), (128, 384), (384, 640), (640, 1024))
 GROUPS = ((0, 256), (256, 512), (512, 768), (768, 896), (896, 1024),)
 SPANS = ((0, 256), (256, 512), (512, 768), (768, 896), (896, 1024),)
-VECTOR_RELUS = (3, 4)
-AHEAD = ((512, 768),)
+VECTOR_RELUS = (3,)
+AHEAD = ((256, 768),)
 
 
 def tile_list_tabres_gelu_kernel(tc, tab_words, tab_scales, w1, w2_words, w2_scales, rT, b, offs, out):
@@ -169,21 +169,21 @@ def tile_list_tabres_gelu_kernel(tc, tab_words, tab_scales, w1, w2_words, w2_sca
         g(640)
         m(5, 5)
         m(6, 6)
+        m(7, 7)
         r(0)
         r(1)
         r(2)
         r(3)
-        p(512)
         q(0)
         y(0, 0)
-        m(7, 7)
         r(4)
         q(256)
-        y(256, 1)
+        p(256)
         r(5)
         r(6)
         e(0)
         r(7)
+        y(256, 1)
         q(512)
         y(512, 2)
         q(768)

@@ -19,14 +19,14 @@ ADD = mybir.AluOpType.add
 P = 128
 PACK = 4
 GROUP = 16
-CHUNK = 128
+CHUNKS = ((0, 128), (128, 256), (256, 384), (384, 512), (512, 576), (576, 640), (640, 768), (768, 896), (896, 1024))
 ROWS_AT = P - 16
 SCALES_AHEAD = 768
 WORD_GATHERS = ((0, 128), (128, 384), (384, 640), (640, 1024))
 GROUPS = ((0, 256), (256, 512), (512, 768), (768, 896), (896, 1024),)
 SPANS = ((0, 256), (256, 512), (512, 768), (768, 896), (896, 1024),)
-VECTOR_RELUS = (3,)
-AHEAD = ((256, 768),)
+VECTOR_RELUS = (384, 512)
+AHEAD = ((512, 768), (896, 1024))
 
 
 def tile_list_tabres_gelu_kernel(tc, tab_words, tab_scales, w1, w2_words, w2_scales, rT, b, offs, out):
@@ -110,19 +110,19 @@ def tile_list_tabres_gelu_kernel(tc, tab_words, tab_scales, w1, w2_words, w2_sca
             hi = dict(WORD_GATHERS)[lo]
             nc.vector.tensor_copy(x_codes[:, lo:hi], tab_words_sb[:].bitcast(U32).indirect(entries(lo, hi)))
 
-        def m(c, bank_no):
-            lo = c * CHUNK
-            bank = banks.tile([P, PACK, CHUNK], F32, name="hbank", tag=f"bank{bank_no}")
-            hbanks[c] = bank
+        def m(lo, bank_no):
+            hi = dict(CHUNKS)[lo]
+            bank = banks.tile([P, PACK, hi - lo], F32, name="hbank", tag=f"bank{bank_no}")
+            hbanks[lo] = bank
             for t in range(PACK):
                 nc.tensor.matmul_mx(out=bank[:, t, :], lhsT=w1_codes[:, t * P:(t + 1) * P].bitcast(FP8X4), lhsT_scale=w1_sc[:, t * P:(t + 1) * P],
-                                    rhs=x_codes[:, lo:lo + CHUNK].bitcast(FP8X4), rhs_scale=x_sc[:, lo:lo + CHUNK], start=True, stop=True)
+                                    rhs=x_codes[:, lo:hi].bitcast(FP8X4), rhs_scale=x_sc[:, lo:hi], start=True, stop=True)
 
-        def r(c):
-            lo = c * CHUNK
-            dst = h_bf[:, PACK * lo:PACK * (lo + CHUNK)].rearrange("p (n t) -> p n t", t=PACK)
-            src = hbanks[c][:].rearrange("p t n -> p n t")
-            if c in VECTOR_RELUS:
+        def r(lo):
+            hi = dict(CHUNKS)[lo]
+            dst = h_bf[:, PACK * lo:PACK * hi].rearrange("p (n t) -> p n t", t=PACK)
+            src = hbanks[lo][:].rearrange("p t n -> p n t")
+            if lo in VECTOR_RELUS:
                 nc.vector.tensor_scalar_max(dst, src, 0.0)
             else:
                 nc.scalar.activation(dst, src, ACT.Relu, bias=relu_bias[:])
@@ -161,37 +161,40 @@ def tile_list_tabres_gelu_kernel(tc, tab_words, tab_scales, w1, w2_words, w2_sca
         g(0)
         m(0, 0)
         g(128)
-        m(1, 1)
-        m(2, 2)
+        m(128, 1)
+        m(256, 2)
         g(384)
-        m(3, 3)
-        m(4, 4)
+        m(384, 3)
+        m(512, 4)
+        m(576, 5)
         g(640)
-        m(5, 5)
-        m(6, 6)
-        m(7, 7)
+        m(640, 6)
+        m(768, 7)
         r(0)
-        r(1)
-        r(2)
-        r(3)
+        r(128)
+        r(256)
+        r(384)
         q(0)
-        y(0, 0)
-        r(4)
+        y(0, 1)
+        m(896, 0)
+        r(512)
         q(256)
-        p(256)
-        r(5)
-        r(6)
+        p(512)
+        p(896)
+        r(576)
+        r(640)
+        r(768)
         e(0)
-        r(7)
-        y(256, 1)
+        r(896)
+        y(256, 2)
         q(512)
-        y(512, 2)
+        y(512, 3)
         q(768)
-        y(768, 3)
+        y(768, 4)
         a(0)
         s(0, 256)
         q(896)
-        y(896, 4)
+        y(896, 5)
         e(256)
         a(256)
         s(256, 512)

from contextlib import ExitStack

import concourse.mybir as mybir

K, H, M, T, S = 512, 512, 128, 2048, 1024
FLOPS = 2 * K * H * S + 2 * H * M * S

F32 = mybir.dt.float32
BF16 = mybir.dt.bfloat16
I32 = mybir.dt.int32
U32 = mybir.dt.uint32
U16 = mybir.dt.uint16
U8 = mybir.dt.uint8
FP8X4 = mybir.dt.float8_e4m3fn_x4
FP4X4 = mybir.dt.float4_e2m1fn_x4
ACT = mybir.ActivationFunctionType
ADD = mybir.AluOpType.add

P = 128
PACK = 4
GROUP = 16
CHUNKS = ((0, 128), (128, 256), (256, 384), (384, 512), (512, 576), (576, 640), (640, 768), (768, 896), (896, 1024))
ROWS_AT = P - 16
SCALES_AHEAD = 768
WORD_GATHERS = ((0, 128), (128, 384), (384, 640), (640, 1024))
GROUPS = ((0, 256), (256, 512), (512, 768), (768, 896), (896, 1024),)
SPANS = ((0, 256), (256, 512), (512, 768), (768, 896), (896, 1024),)
VECTOR_RELUS = (384, 512)
AHEAD = ((512, 768), (896, 1024))


def tile_list_tabres_gelu_kernel(tc, tab_words, tab_scales, w1, w2_words, w2_scales, rT, b, offs, out):
    nc = tc.nc
    with ExitStack() as ctx:
        keep = ctx.enter_context(tc.tile_pool(name="keep", bufs=1))
        late = ctx.enter_context(tc.tile_pool(name="late", bufs=1))
        banks = ctx.enter_context(tc.psum_pool(name="banks", bufs=1))

        offsets = keep.tile([P, S // GROUP], U16, name="offsets")
        tab_words_sb = keep.tile([P, T], I32, name="tab_words_sb", align_bytes=64)
        w1_raw = keep.tile([P, PACK, H], F32, name="w1_raw")
        w1_bf = keep.tile([P, PACK * H], BF16, name="w1_bf", align_bytes=64)
        w1_codes = keep.tile([P, H], U32, name="w1_codes", align_bytes=64)
        w1_sc = keep.tile([P, H], U8, name="w1_sc", align_bytes=64)
        zero = keep.tile([P, 1], F32, name="zero")
        relu_bias = keep.tile([P, 1], F32, name="relu_bias")
        x_codes = keep.tile([P, S], U32, name="x_codes", align_bytes=64)
        x_sc_rows = keep.tile([P, S], U8, name="x_sc_rows", align_bytes=64)
        staged = keep.tile([P, S - SCALES_AHEAD + M], U8, name="staged", align_bytes=64)
        x_sc = keep.tile([P, S + M], U8, name="x_sc", align_bytes=64)
        h_bf = keep.tile([P, PACK * S], BF16, name="h_bf", align_bytes=64)
        h_codes = keep.tile([P, S], U32, name="h_codes", align_bytes=64)
        h_sc = keep.tile([P, S], U8, name="h_sc", align_bytes=64)
        res = keep.tile([P, S], F32, name="res", align_bytes=64)
        act = keep.tile([P, S], F32, name="act", align_bytes=64)
        fin = keep.tile([P, S], F32, name="fin", align_bytes=64)

        tab_scales_sb = late.tile([P, T // 4], I32, name="tab_scales_sb", align_bytes=64, offset=4 * T - T // 2)
        rT_sb = late.tile([P, T], F32, name="rT_sb", align_bytes=64, offset=0)
        w2_codes = late.tile([P, 2 * M], U8, name="w2_codes", align_bytes=64, offset=4 * T)
        bias = late.tile([P, 1], F32, name="bias", align_bytes=64, offset=4 * T + 2 * M)

        def entries(lo, hi):
            return offsets[:, lo // GROUP:hi // GROUP]

        nc.vector.memset(tab_scales_sb[:ROWS_AT, :], 0)
        nc.vector.memset(zero[:], 0.0)
        nc.vector.memset(x_sc[:].bitcast(I32), 0)
        nc.scalar.activation(relu_bias[:], zero[:], ACT.Gelu_apprx_tanh)

        words = tab_words[0].rearrange("p t i -> p (t i)").bitcast(I32)
        nc.scalar.dma_start(tab_scales_sb[ROWS_AT:ROWS_AT + 16, :], tab_scales[0].bitcast(I32))
        nc.sync.dma_start(offsets[:], offs)
        nc.sync.dma_start(w1_raw[:], w1.rearrange("(p j) c -> p j c", j=PACK))
        nc.sync.dma_start(staged[:].bitcast(I32)[ROWS_AT:, (S - SCALES_AHEAD) // 4:], w2_scales[0].bitcast(I32))
        nc.sync.dma_start(tab_words_sb[:, :512], words[:, :512])
        nc.sync.dma_start(tab_words_sb[:, 512:], words[:, 512:])

        def move_scales(dst, src):
            for q in range(4):
                nc.sync.dma_start(dst[32 * q:32 * q + 4, :], src[ROWS_AT + 4 * q:ROWS_AT + 4 * q + 4, :])

        for lo, hi in ((0, 768), (768, S)):
            nc.vector.tensor_copy(x_sc_rows[:, lo:hi], tab_scales_sb[:].bitcast(U8).indirect(entries(lo, hi)))
        ahead = SCALES_AHEAD // 4
        move_scales(x_sc[:].bitcast(I32)[:, :ahead], x_sc_rows[:].bitcast(I32)[:, :ahead])
        nc.sync.dma_start(rT_sb[:], rT)
        nc.sync.dma_start(w2_codes[:].bitcast(I32), w2_words[0].bitcast(I32))
        with nc.allow_non_contiguous_dma(reason="one bias value a partition"):
            nc.sync.dma_start(bias[:], b.rearrange("(p o) -> p o", o=1))
        nc.vector.tensor_copy(staged[:].bitcast(I32)[:, :S // 4 - ahead], x_sc_rows[:].bitcast(I32)[:, ahead:])
        move_scales(x_sc[:].bitcast(I32)[:, ahead:], staged[:].bitcast(I32))

        w1_dst = w1_bf[:].rearrange("p (t m j) -> p m j t", t=PACK, j=PACK)
        w1_src = w1_raw[:].rearrange("p j (m t) -> p m j t", t=PACK)
        nc.scalar.copy(w1_dst[:, :, :, 0:2], w1_src[:, :, :, 0:2])
        nc.vector.tensor_copy(w1_dst[:, :, :, 2:4], w1_src[:, :, :, 2:4])
        for lo in range(0, H, 2 * P):
            hi = lo + 2 * P
            nc.vector.quantize_mx(out=w1_codes[:, lo:hi].bitcast(FP8X4), scales=w1_sc[:, lo:hi], in_=w1_bf[:, PACK * lo:PACK * hi])

        hbanks = {}
        ybanks = {}
        warm = banks.tile([P, 512], F32, name="warm", tag="bank7")
        for rep in range(3):
            nc.tensor.matmul_mx(out=warm[:32, :], lhsT=tab_words_sb[:, :32].bitcast(FP8X4), lhsT_scale=x_sc_rows[:, :32],
                                rhs=tab_words_sb[:, :512].bitcast(FP8X4), rhs_scale=x_sc_rows[:, :512], start=True, stop=True)

        def g(lo):
            hi = dict(WORD_GATHERS)[lo]
            nc.vector.tensor_copy(x_codes[:, lo:hi], tab_words_sb[:].bitcast(U32).indirect(entries(lo, hi)))

        def m(lo, bank_no):
            hi = dict(CHUNKS)[lo]
            bank = banks.tile([P, PACK, hi - lo], F32, name="hbank", tag=f"bank{bank_no}")
            hbanks[lo] = bank
            for t in range(PACK):
                nc.tensor.matmul_mx(out=bank[:, t, :], lhsT=w1_codes[:, t * P:(t + 1) * P].bitcast(FP8X4), lhsT_scale=w1_sc[:, t * P:(t + 1) * P],
                                    rhs=x_codes[:, lo:hi].bitcast(FP8X4), rhs_scale=x_sc[:, lo:hi], start=True, stop=True)

        def r(lo):
            hi = dict(CHUNKS)[lo]
            dst = h_bf[:, PACK * lo:PACK * hi].rearrange("p (n t) -> p n t", t=PACK)
            src = hbanks[lo][:].rearrange("p t n -> p n t")
            if lo in VECTOR_RELUS:
                nc.vector.tensor_scalar_max(dst, src, 0.0)
            else:
                nc.scalar.activation(dst, src, ACT.Relu, bias=relu_bias[:])

        def p(lo):
            hi = dict(AHEAD)[lo]
            nc.vector.tensor_copy(res[:, lo:hi], rT_sb[:].indirect(entries(lo, hi)))

        def q(lo):
            hi = dict(GROUPS)[lo]
            nc.vector.quantize_mx(out=h_codes[:, lo:hi].bitcast(FP8X4), scales=h_sc[:, lo:hi], in_=h_bf[:, PACK * lo:PACK * hi])

        def y(lo, bank_no):
            hi = dict(GROUPS)[lo]
            codes = h_codes[:, lo:hi].bitcast(FP8X4)
            ybank = banks.tile([P, hi - lo], F32, name="ybank", tag=f"bank{bank_no}")
            ybanks[lo] = ybank
            nc.tensor.matmul_mx(out=ybank[:], lhsT=w2_codes[:].bitcast(FP4X4), lhsT_scale=x_sc[:, S:],
                                rhs=codes, rhs_scale=h_sc[:, lo:hi], start=True, stop=True)

        def e(lo):
            hi = dict(SPANS)[lo]
            first = max(a for a, z in GROUPS if a <= lo)
            nc.scalar.activation(act[:, lo:hi], ybanks[first][:, lo - first:hi - first], ACT.Gelu_apprx_tanh, bias=bias[:])

        def a(lo):
            hi = dict(SPANS)[lo]
            if any(x <= lo < z for x, z in AHEAD):
                nc.vector.tensor_tensor(fin[:, lo:hi], act[:, lo:hi], res[:, lo:hi], ADD)
            else:
                nc.vector.tensor_tensor(fin[:, lo:hi], rT_sb[:].indirect(entries(lo, hi)), act[:, lo:hi], ADD)

        def s(lo, hi):
            nc.sync.dma_start(out[:, lo:hi], fin[:, lo:hi])

        g(0)
        m(0, 0)
        g(128)
        m(128, 1)
        m(256, 2)
        g(384)
        m(384, 3)
        m(512, 4)
        m(576, 5)
        g(640)
        m(640, 6)
        m(768, 7)
        r(0)
        r(128)
        r(256)
        r(384)
        q(0)
        y(0, 1)
        m(896, 0)
        r(512)
        q(256)
        p(512)
        p(896)
        r(576)
        r(640)
        r(768)
        e(0)
        r(896)
        y(256, 2)
        q(512)
        y(512, 3)
        q(768)
        y(768, 4)
        a(0)
        s(0, 256)
        q(896)
        y(896, 5)
        e(256)
        a(256)
        s(256, 512)
        e(512)
        a(512)
        s(512, 768)
        e(768)
        a(768)
        s(768, 896)
        e(896)
        a(896)
        s(896, 1024)
